import numpy as np
import ml_dtypes


def mxq(x, axis, fmt="e4m3"):
    dtype, down = {"e4m3": (ml_dtypes.float8_e4m3fn, 7), "e5m2": (ml_dtypes.float8_e5m2, 14)}[fmt]
    v = np.moveaxis(np.asarray(x, np.float32).astype(ml_dtypes.bfloat16).astype(np.float64), axis, -1)
    blocks = v.reshape(v.shape[:-1] + (-1, 32))
    amax = np.abs(blocks).max(-1, keepdims=True)
    byte = np.maximum(np.where(amax > 0, np.frexp(amax)[1] - 1 + 127, 0) - down, 1)
    scale = np.exp2(byte - 127.0)
    codes = (blocks / scale).astype(np.float32).astype(dtype).astype(np.float64)
    return np.moveaxis((codes * scale).reshape(v.shape), -1, axis)


WIDE = False


def mx_kscale(k):
    if not WIDE:
        return np.ones(k)
    levels = np.array([10, -10, 5, -5, 0])
    if k % 512:
        return np.exp2(np.random.permutation(np.resize(levels, k // 32))).repeat(32)
    a = np.empty((k // 512, 16))
    for p in range(k // 512):
        a[p, :8] = np.random.permutation(np.resize(levels, 8))
        for g in range(8):
            far = levels[np.abs(levels - a[p, g]) >= 10]
            a[p, g + 8] = far[np.random.randint(len(far))]
    return np.exp2(a.ravel()).repeat(32)


def f64(x):
    return np.asarray(x).astype(np.float64)


def striped(idx):
    return np.tile(np.asarray(idx).reshape(-1, 16).T, (8, 1)).astype(np.uint16)


def unstriped(offs):
    return offs[:16].T.reshape(-1).astype(np.int64)


def bf(x):
    return np.asarray(x, np.float32).astype(ml_dtypes.bfloat16)


def planes(Y):
    r, m = Y.shape
    b = f64(bf(Y)).reshape(r // 32, 32, m)
    amax = np.abs(b).max(1)
    byte = np.clip(np.where(amax > 0, np.frexp(amax)[1] - 1 + 127 - 7, 1), 1, 254)
    codes = (b * np.exp2(127.0 - byte)[:, None, :]).reshape(r, m).astype(np.float32).astype(ml_dtypes.float8_e4m3fn).view(np.uint8)
    words = codes.reshape(r // 512, 128, 4, m).transpose(0, 1, 3, 2)
    return np.ascontiguousarray(words), np.ascontiguousarray(byte.astype(np.uint8).reshape(r // 512, 16, m))


D, T, I, G, U, Q = 512, 2048, 1024, 128, 512, 512


def setup_inputs():
    n = np.random.standard_normal
    idx = np.random.permutation(T)[:I]
    idx2 = np.random.permutation(U)[:G]
    fd = mx_kscale(D)
    return {
        "query": (n((D, Q)) * 0.5 / np.sqrt(D) * fd[:, None]).astype(np.float32),
        "keys": (n((D, T))).astype(np.float32),
        "sg": (np.random.uniform(-1.0, 1.0, (1, I))).astype(np.float32),
        "dsc": (np.random.uniform(0.5, 1.5, (D, 1)) / fd[:, None]).astype(np.float32),
        "bias": (0.5 * n((Q, U))).astype(np.float32),
        "offs": striped(idx),
        "offs2": striped(idx2),
    }


def reference(query, keys, sg, dsc, bias, offs, offs2):
    idx = unstriped(offs)
    idx2 = unstriped(offs2)
    sk = (f64(keys)[:, idx] * f64(sg)).reshape(D, G, I // G).sum(axis=2) * f64(dsc)
    queryq = mxq(f64(query), 0, "e4m3")
    skq = mxq(sk, 0, "e4m3")
    a = queryq.T @ skq
    s = a + f64(bias)[:, idx2]
    p = np.exp(s - np.max(s, axis=1, keepdims=True))
    y = p / np.sum(p, axis=1, keepdims=True) * 128.0
    words, scales = planes(y)
    return y, words, scales

@@ -1,0 +1,146 @@
+from contextlib import ExitStack
+
+import concourse.mybir as mybir
+from concourse.masks import make_identity
+
+D, T, I, G, U, Q = 512, 2048, 1024, 128, 512, 512
+FLOPS = 2 * D * Q * G
+
+F32 = mybir.dt.float32
+BF16 = mybir.dt.bfloat16
+U32 = mybir.dt.uint32
+U16 = mybir.dt.uint16
+I32 = mybir.dt.int32
+U8 = mybir.dt.uint8
+FP8X4 = mybir.dt.float8_e4m3fn_x4
+ALU = mybir.AluOpType
+ACT = mybir.ActivationFunctionType
+AX = mybir.AxisListType
+
+P = 128
+PACK = 4
+PAGE = I // G
+PATHS = [2,2,2,1]
+
+
+def tile_attend_pagesketch_pl_kernel(tc, query, keys, sg, dsc, bias, offs, offs2, out_0, out_1, out_2):
+    nc = tc.nc
+    with ExitStack() as ctx:
+        keep = ctx.enter_context(tc.tile_pool(name="keep", bufs=1))
+        psum = ctx.enter_context(tc.psum_pool(name="psum", bufs=1))
+
+        keys_v = keys.rearrange("(p t) n -> p t n", t=PACK)
+        query_v = query.rearrange("(p t) n -> p t n", t=PACK)
+        bias_v = bias.rearrange("(p r) n -> p r n", r=PACK)
+
+        kt = [keep.tile([P, T], F32, name="keys%d" % t) for t in range(PACK)]
+        offs_sb = keep.tile([P, I // 16], U16, name="offs_sb")
+        offs2_sb = keep.tile([P, G // 16], U16, name="offs2_sb")
+        sg_col = keep.tile([P, PAGE], F32, name="sg_col")
+        dsc_sb = keep.tile([P, PACK], F32, name="dsc_sb")
+        qraw = [keep.tile([P, PACK, Q // 2], F32, name="qraw%d" % h) for h in range(2)]
+        bt = [keep.tile([P, U], F32, name="bias%d" % r) for r in range(PACK)]
+
+        nc.sync.dma_start(sg_col[:], sg.rearrange("o (p j) -> p (o j)", j=PAGE))
+        nc.sync.dma_start(kt[0][:], keys_v[:, 0, :])
+        nc.sync.dma_start(offs_sb[:], offs)
+        nc.sync.dma_start(dsc_sb[:], dsc.rearrange("(p t) o -> p (t o)", t=PACK))
+        for t in range(1, PACK):
+            nc.sync.dma_start(kt[t][:], keys_v[:, t, :])
+        nc.sync.dma_start(offs2_sb[:], offs2)
+        for h in range(2):
+            nc.sync.dma_start(qraw[h][:], query_v[:, :, h * (Q // 2):(h + 1) * (Q // 2)])
+        for r in range(PACK):
+            nc.sync.dma_start(bt[r][:], bias_v[:, r, :])
+
+        ident = keep.tile([P, P], F32, name="ident")
+        make_identity(nc, ident[:])
+        warm = keep.tile([P, 1], F32, name="warm")
+        nc.scalar.activation(warm[:], ident[:, 0:1], ACT.Exp)
+
+        sgb = keep.tile([P, G, PAGE], F32, name="sgb")
+        sgb3 = keep.tile([P, G, PAGE], F32, name="sgb3")
+        sgps = [psum.tile([P, 4, G], F32, name="sgps%d" % a, tag="w%d" % a) for a in range(2)]
+        for a in range(2):
+            for j in range(4):
+                nc.tensor.transpose(sgps[a][:, j, :], sg_col[:, 4 * a + j:4 * a + j + 1].to_broadcast([P, P]), ident[:])
+        nc.scalar.copy(sgb[:, :, 0:4], sgps[0][:].rearrange("p j g -> p g j"))
+        nc.vector.tensor_copy(sgb[:, :, 4:8], sgps[1][:].rearrange("p j g -> p g j"))
+        for a in range(2):
+            nc.scalar.activation(sgb3[:, :, 4 * a:4 * a + 4], sgps[a][:].rearrange("p j g -> p g j"), ACT.Copy,
+                                 scale=dsc_sb[:, 3:4])
+
+        skf = keep.tile([P, PACK, G], F32, name="skf")
+        skb = keep.tile([P, G, PACK], BF16, name="skb", align_bytes=64)
+        for t in range(PACK):
+            gat = keep.tile([P, G, PAGE], F32, name="gat%d" % t)
+            gflat = gat[:].rearrange("p g j -> p (g j)")
+            win = kt[t][:].indirect(offs_sb[:])
+            if PATHS[t] == 1:
+                nc.vector.tensor_tensor(gflat, win, sgb3[:].rearrange("p g j -> p (g j)"), ALU.mult)
+                nc.vector.tensor_reduce(skf[:, t, :], gat[:], AX.X, ALU.add)
+            elif PATHS[t] == 2:
+                nc.vector.tensor_tensor(gflat, win, sgb[:].rearrange("p g j -> p (g j)"), ALU.mult)
+                red = psum.tile([P, P], F32, name="red%d" % t, tag="r%d" % (t % 2))
+                for j in range(PAGE):
+                    nc.tensor.matmul(red[:], gat[:, :, j], ident[:], start=(j == 0), stop=(j == PAGE - 1),
+                                     is_transpose=True)
+                reds = keep.tile([P, P], F32, name="reds%d" % t)
+                nc.scalar.copy(reds[:], red[:])
+                skT = psum.tile([P, G], F32, name="skT%d" % t, tag="skT")
+                nc.tensor.transpose(skT[:], reds[:], ident[:])
+                nc.scalar.activation(skf[:, t, :], skT[:], ACT.Copy, scale=dsc_sb[:, t:t + 1])
+
+        qb = keep.tile([P, PACK, P, PACK], BF16, name="qb", align_bytes=64)
+        for h in range(2):
+            dst = qb[:, :, h * 64:(h + 1) * 64, :].rearrange("p r m j -> p m j r")
+            src = qraw[h][:].rearrange("p j (m r) -> p m j r", r=PACK)
+            nc.scalar.copy(dst, src)
+        qc = keep.tile([P, Q], U32, name="qc", align_bytes=64)
+        qs = keep.tile([P, Q], U8, name="qs", align_bytes=64)
+        nc.vector.quantize_mx(out=qc[:].bitcast(FP8X4), scales=qs[:], in_=qb[:].rearrange("p r m j -> p (r m j)"))
+
+        nc.scalar.copy(skb[:].rearrange("p (c i) t -> p c t i", i=4), skf[:].rearrange("p t (c i) -> p c t i", i=4))
+        bg = keep.tile([P, PACK, G], F32, name="bg")
+        nc.vector.tensor_copy(bg[:, 0, :], bt[0][:].indirect(offs2_sb[:]))
+        skc = keep.tile([P, G], U32, name="skc", align_bytes=64)
+        sks = keep.tile([P, G], U8, name="sks", align_bytes=64)
+        nc.vector.quantize_mx(out=skc[:].bitcast(FP8X4), scales=sks[:], in_=skb[:].rearrange("p g t -> p (g t)"))
+        for r in range(1, PACK):
+            nc.vector.tensor_copy(bg[:, r, :], bt[r][:].indirect(offs2_sb[:]))
+
+        acc = [psum.tile([P, G], F32, name="acc%d" % r, tag=["w0", "w1", "a2", "a3"][r]) for r in range(PACK)]
+        for r in range(PACK):
+            cols = slice(r * P, (r + 1) * P)
+            nc.tensor.matmul_mx(out=acc[r][:], lhsT=qc[:, cols].bitcast(FP8X4), lhsT_scale=qs[:, cols],
+                                rhs=skc[:].bitcast(FP8X4), rhs_scale=sks[:], start=True, stop=True)
+
+        s = keep.tile([P, PACK, G], F32, name="s")
+        nmax = keep.tile([P, PACK], F32, name="nmax")
+        pe = keep.tile([P, PACK, G], F32, name="pe")
+        ssum = keep.tile([P, PACK], F32, name="ssum")
+        rinv = keep.tile([P, PACK], F32, name="rinv")
+        y = keep.tile([P, PACK, G], F32, name="y")
+        yb = keep.tile([P, G, PACK], BF16, name="yb", align_bytes=64)
+        yc = keep.tile([P, G], U32, name="yc", align_bytes=64)
+        ys = keep.tile([P, G], U8, name="ys", align_bytes=64)
+        for r in range(PACK + 1):
+            if r < PACK:
+                nc.vector.tensor_tensor(s[:, r, :], acc[r][:], bg[:, r, :], ALU.add)
+            if r > 0:
+                k = r - 1
+                nc.vector.tensor_reduce(nmax[:, k:k + 1], s[:, k, :], AX.X, ALU.max, negate=True)
+                nc.scalar.activation(pe[:, k, :], s[:, k, :], ACT.Exp, bias=nmax[:, k:k + 1],
+                                     accum_out=ssum[:, k:k + 1])
+        nc.vector.reciprocal(rinv[:], ssum[:])
+        nc.vector.scalar_tensor_tensor(yb[:], pe[:].rearrange("p r g -> p g r"), 128.0,
+                                       rinv[:].unsqueeze(1).to_broadcast([P, G, PACK]), ALU.mult, ALU.mult)
+        for r in range(PACK):
+            nc.vector.tensor_scalar(y[:, r, :], pe[:, r, :], 128.0, rinv[:, r:r + 1], ALU.mult, ALU.mult)
+        nc.vector.quantize_mx(out=yc[:].bitcast(FP8X4), scales=ys[:], in_=yb[:].rearrange("p g r -> p (g r)"))
+
+        nc.sync.dma_start(out_0.rearrange("(p r) g -> p r g", r=PACK), y[:])
+        nc.scalar.dma_start(out_1.rearrange("z l c r -> l (z c r)").bitcast(I32), yc[:].bitcast(I32))
+        for k in range(4):
+            eng = nc.sync if k % 2 == 0 else nc.scalar
+            eng.dma_start(out_2[0, 4 * k:4 * k + 4, :].bitcast(I32), ys[32 * k:32 * k + 4, :].bitcast(I32))

@@ -38,20 +38,23 @@ def tile_attend_pagesketch_pl_kernel(tc, query, keys, sg, dsc, bias, offs, offs2
         offs2_sb = keep.tile([P, G // 16], U16, name="offs2_sb")
         sg_col = keep.tile([P, PAGE], F32, name="sg_col")
         dsc_sb = keep.tile([P, PACK], F32, name="dsc_sb")
-        qraw = [keep.tile([P, PACK, Q // 2], F32, name="qraw%d" % h) for h in range(2)]
+        qraw = [keep.tile([P, PACK, Q // 2], F32, name="qraw%d" % h, tag="qraw%d" % h) for h in range(2)]
         bt = [keep.tile([P, U], F32, name="bias%d" % r) for r in range(PACK)]
 
         nc.sync.dma_start(sg_col[:], sg.rearrange("o (p j) -> p (o j)", j=PAGE))
         nc.sync.dma_start(kt[0][:], keys_v[:, 0, :])
         nc.sync.dma_start(offs_sb[:], offs)
         nc.sync.dma_start(dsc_sb[:], dsc.rearrange("(p t) o -> p (t o)", t=PACK))
-        for t in range(1, PACK):
-            nc.sync.dma_start(kt[t][:], keys_v[:, t, :])
+        nc.sync.dma_start(kt[1][:], keys_v[:, 1, :])
+        nc.sync.dma_start(kt[2][:], keys_v[:, 2, :])
+        nc.sync.dma_start(qraw[0][:], query_v[:, :, 0:256])
+        nc.sync.dma_start(kt[3][:], keys_v[:, 3, :])
         nc.sync.dma_start(offs2_sb[:], offs2)
-        for h in range(2):
-            nc.sync.dma_start(qraw[h][:], query_v[:, :, h * (Q // 2):(h + 1) * (Q // 2)])
-        for r in range(PACK):
-            nc.sync.dma_start(bt[r][:], bias_v[:, r, :])
+        nc.sync.dma_start(qraw[1][:], query_v[:, :, 256:512])
+        nc.sync.dma_start(bt[0][:], bias_v[:, 0, :])
+        nc.sync.dma_start(bt[1][:], bias_v[:, 1, :])
+        nc.sync.dma_start(bt[2][:], bias_v[:, 2, :])
+        nc.sync.dma_start(bt[3][:], bias_v[:, 3, :])
 
         ident = keep.tile([P, P], F32, name="ident")
         make_identity(nc, ident[:])
@@ -70,8 +73,13 @@ def tile_attend_pagesketch_pl_kernel(tc, query, keys, sg, dsc, bias, offs, offs2
             nc.scalar.activation(sgb3[:, :, 4 * a:4 * a + 4], sgps[a][:].rearrange("p j g -> p g j"), ACT.Copy,
                                  scale=dsc_sb[:, 3:4])
 
+        qb = keep.tile([P, PACK, P, PACK], BF16, name="qb", align_bytes=64)
+        for h in range(2):
+            dst = qb[:, :, h * 64:(h + 1) * 64, :].rearrange("p r m j -> p m j r")
+            src = qraw[h][:].rearrange("p j (m r) -> p m j r", r=PACK)
+            nc.scalar.copy(dst, src)
         skf = keep.tile([P, PACK, G], F32, name="skf")
-        skb = keep.tile([P, G, PACK], BF16, name="skb", align_bytes=64)
+        skb = keep.tile([P, G, PACK], BF16, name="skb", tag="skb", align_bytes=64)
         for t in range(PACK):
             gat = keep.tile([P, G, PAGE], F32, name="gat%d" % t)
             gflat = gat[:].rearrange("p g j -> p (g j)")
@@ -85,29 +93,26 @@ def tile_attend_pagesketch_pl_kernel(tc, query, keys, sg, dsc, bias, offs, offs2
                 for j in range(PAGE):
                     nc.tensor.matmul(red[:], gat[:, :, j], ident[:], start=(j == 0), stop=(j == PAGE - 1),
                                      is_transpose=True)
-                reds = keep.tile([P, P], F32, name="reds%d" % t)
+                reds = keep.tile([P, P], F32, name="reds%d" % t, tag=("qraw1" if t == 2 else "reds%d" % t))
                 nc.scalar.copy(reds[:], red[:])
                 skT = psum.tile([P, G], F32, name="skT%d" % t, tag="skT")
                 nc.tensor.transpose(skT[:], reds[:], ident[:])
                 nc.scalar.activation(skf[:, t, :], skT[:], ACT.Copy, scale=dsc_sb[:, t:t + 1])
 
-        qb = keep.tile([P, PACK, P, PACK], BF16, name="qb", align_bytes=64)
-        for h in range(2):
-            dst = qb[:, :, h * 64:(h + 1) * 64, :].rearrange("p r m j -> p m j r")
-            src = qraw[h][:].rearrange("p j (m r) -> p m j r", r=PACK)
-            nc.scalar.copy(dst, src)
         qc = keep.tile([P, Q], U32, name="qc", align_bytes=64)
         qs = keep.tile([P, Q], U8, name="qs", align_bytes=64)
         nc.vector.quantize_mx(out=qc[:].bitcast(FP8X4), scales=qs[:], in_=qb[:].rearrange("p r m j -> p (r m j)"))
 
         nc.scalar.copy(skb[:].rearrange("p (c i) t -> p c t i", i=4), skf[:].rearrange("p t (c i) -> p c t i", i=4))
-        bg = keep.tile([P, PACK, G], F32, name="bg")
-        nc.vector.tensor_copy(bg[:, 0, :], bt[0][:].indirect(offs2_sb[:]))
+        bg = [keep.tile([P, G], F32, name="bg%d" % r) for r in range(3)]
+        for r in range(3):
+            nc.vector.tensor_copy(bg[r][:], bt[r][:].indirect(offs2_sb[:]))
         skc = keep.tile([P, G], U32, name="skc", align_bytes=64)
         sks = keep.tile([P, G], U8, name="sks", align_bytes=64)
         nc.vector.quantize_mx(out=skc[:].bitcast(FP8X4), scales=sks[:], in_=skb[:].rearrange("p g t -> p (g t)"))
-        for r in range(1, PACK):
-            nc.vector.tensor_copy(bg[:, r, :], bt[r][:].indirect(offs2_sb[:]))
+        bgl = keep.tile([P, 1, G], F32, name="bgl", tag="skb", align_bytes=64)
+        for r in range(3, PACK):
+            nc.vector.tensor_copy(bgl[:, r - 3, :], bt[r][:].indirect(offs2_sb[:]))
 
         acc = [psum.tile([P, G], F32, name="acc%d" % r, tag=["w0", "w1", "a2", "a3"][r]) for r in range(PACK)]
         for r in range(PACK):
@@ -126,20 +131,23 @@ def tile_attend_pagesketch_pl_kernel(tc, query, keys, sg, dsc, bias, offs, offs2
         ys = keep.tile([P, G], U8, name="ys", align_bytes=64)
         for r in range(PACK + 1):
             if r < PACK:
-                nc.vector.tensor_tensor(s[:, r, :], acc[r][:], bg[:, r, :], ALU.add)
+                nc.vector.tensor_tensor(s[:, r, :], acc[r][:], (bg[r][:] if r < 3 else bgl[:, r - 3, :]), ALU.add)
             if r > 0:
                 k = r - 1
                 nc.vector.tensor_reduce(nmax[:, k:k + 1], s[:, k, :], AX.X, ALU.max, negate=True)
                 nc.scalar.activation(pe[:, k, :], s[:, k, :], ACT.Exp, bias=nmax[:, k:k + 1],
                                      accum_out=ssum[:, k:k + 1])
-        nc.vector.reciprocal(rinv[:], ssum[:])
-        nc.vector.scalar_tensor_tensor(yb[:], pe[:].rearrange("p r g -> p g r"), 128.0,
-                                       rinv[:].unsqueeze(1).to_broadcast([P, G, PACK]), ALU.mult, ALU.mult)
-        for r in range(PACK):
-            nc.vector.tensor_scalar(y[:, r, :], pe[:, r, :], 128.0, rinv[:, r:r + 1], ALU.mult, ALU.mult)
+        out_v = out_0.rearrange("(p r) g -> p r g", r=PACK)
+        for h in range(2):
+            rr = slice(2 * h, 2 * h + 2)
+            nc.vector.reciprocal(rinv[:, rr], ssum[:, rr])
+            nc.vector.scalar_tensor_tensor(yb[:, :, rr], pe[:, rr, :].rearrange("p r g -> p g r"), 128.0,
+                                           rinv[:, rr].unsqueeze(1).to_broadcast([P, G, 2]), ALU.mult, ALU.mult)
+            for r in range(2 * h, 2 * h + 2):
+                nc.vector.tensor_scalar(y[:, r, :], pe[:, r, :], 128.0, rinv[:, r:r + 1], ALU.mult, ALU.mult)
+            nc.sync.dma_start(out_v[:, rr, :], y[:, rr, :])
         nc.vector.quantize_mx(out=yc[:].bitcast(FP8X4), scales=ys[:], in_=yb[:].rearrange("p g r -> p (g r)"))
 
-        nc.sync.dma_start(out_0.rearrange("(p r) g -> p r g", r=PACK), y[:])
         nc.scalar.dma_start(out_1.rearrange("z l c r -> l (z c r)").bitcast(I32), yc[:].bitcast(I32))
         for k in range(4):
             eng = nc.sync if k % 2 == 0 else nc.scalar

@@ -20,124 +20,213 @@ AX = mybir.AxisListType
 P = 128
 PACK = 4
 PAGE = I // G
-PATHS = [2,2,2,1]
+TAGS = {"reds2":"qraw1","bg2":"skb","bg3":"gat3","qb":"sg_col"}
 
 
 def tile_attend_pagesketch_pl_kernel(tc, query, keys, sg, dsc, bias, offs, offs2, out_0, out_1, out_2):
     nc = tc.nc
     with ExitStack() as ctx:
+        lists = ctx.enter_context(tc.tile_pool(name="lists", bufs=1))
         keep = ctx.enter_context(tc.tile_pool(name="keep", bufs=1))
         psum = ctx.enter_context(tc.psum_pool(name="psum", bufs=1))
+
+        def sb(shape, dtype, name):
+            return keep.tile(shape, dtype, name=name, tag=TAGS.get(name, name), align_bytes=64)
+
+        def ps(shape, name, tag):
+            return psum.tile(shape, F32, name=name, tag=tag)
 
         keys_v = keys.rearrange("(p t) n -> p t n", t=PACK)
         query_v = query.rearrange("(p t) n -> p t n", t=PACK)
         bias_v = bias.rearrange("(p r) n -> p r n", r=PACK)
+        out_v = out_0.rearrange("(p r) g -> p r g", r=PACK)
 
-        kt = [keep.tile([P, T], F32, name="keys%d" % t) for t in range(PACK)]
-        offs_sb = keep.tile([P, I // 16], U16, name="offs_sb")
-        offs2_sb = keep.tile([P, G // 16], U16, name="offs2_sb")
-        sg_col = keep.tile([P, PAGE], F32, name="sg_col")
-        dsc_sb = keep.tile([P, PACK], F32, name="dsc_sb")
-        qraw = [keep.tile([P, PACK, Q // 2], F32, name="qraw%d" % h, tag="qraw%d" % h) for h in range(2)]
-        bt = [keep.tile([P, U], F32, name="bias%d" % r) for r in range(PACK)]
+        kt = [sb([P, T], F32, "keys%d" % t) for t in range(PACK)]
+        offs_sb = lists.tile([P, I // 16], U16, name="offs_sb")
+        offs2_sb = lists.tile([P, G // 16], U16, name="offs2_sb")
+        sg_col = sb([P, PAGE], F32, "sg_col")
+        dsc_sb = sb([P, PACK], F32, "dsc_sb")
+        qraw = [sb([P, PACK, Q // 2], F32, "qraw%d" % h) for h in range(2)]
+        bt = [sb([P, U], F32, "bias%d" % r) for r in range(PACK)]
 
-        nc.sync.dma_start(sg_col[:], sg.rearrange("o (p j) -> p (o j)", j=PAGE))
         nc.sync.dma_start(kt[0][:], keys_v[:, 0, :])
         nc.sync.dma_start(offs_sb[:], offs)
+        nc.sync.dma_start(sg_col[:], sg.rearrange("o (p j) -> p (o j)", j=PAGE))
         nc.sync.dma_start(dsc_sb[:], dsc.rearrange("(p t) o -> p (t o)", t=PACK))
         nc.sync.dma_start(kt[1][:], keys_v[:, 1, :])
         nc.sync.dma_start(kt[2][:], keys_v[:, 2, :])
-        nc.sync.dma_start(qraw[0][:], query_v[:, :, 0:256])
         nc.sync.dma_start(kt[3][:], keys_v[:, 3, :])
         nc.sync.dma_start(offs2_sb[:], offs2)
+        nc.sync.dma_start(qraw[0][:], query_v[:, :, 0:256])
         nc.sync.dma_start(qraw[1][:], query_v[:, :, 256:512])
         nc.sync.dma_start(bt[0][:], bias_v[:, 0, :])
         nc.sync.dma_start(bt[1][:], bias_v[:, 1, :])
         nc.sync.dma_start(bt[2][:], bias_v[:, 2, :])
         nc.sync.dma_start(bt[3][:], bias_v[:, 3, :])
 
-        ident = keep.tile([P, P], F32, name="ident")
+        ident = sb([P, P], F32, "ident")
         make_identity(nc, ident[:])
-        warm = keep.tile([P, 1], F32, name="warm")
+        warm = sb([P, 1], F32, "warm")
         nc.scalar.activation(warm[:], ident[:, 0:1], ACT.Exp)
 
-        sgb = keep.tile([P, G, PAGE], F32, name="sgb")
-        sgb3 = keep.tile([P, G, PAGE], F32, name="sgb3")
-        sgps = [psum.tile([P, 4, G], F32, name="sgps%d" % a, tag="w%d" % a) for a in range(2)]
-        for a in range(2):
-            for j in range(4):
-                nc.tensor.transpose(sgps[a][:, j, :], sg_col[:, 4 * a + j:4 * a + j + 1].to_broadcast([P, P]), ident[:])
-        nc.scalar.copy(sgb[:, :, 0:4], sgps[0][:].rearrange("p j g -> p g j"))
-        nc.vector.tensor_copy(sgb[:, :, 4:8], sgps[1][:].rearrange("p j g -> p g j"))
-        for a in range(2):
-            nc.scalar.activation(sgb3[:, :, 4 * a:4 * a + 4], sgps[a][:].rearrange("p j g -> p g j"), ACT.Copy,
-                                 scale=dsc_sb[:, 3:4])
+        tl = {}
 
-        qb = keep.tile([P, PACK, P, PACK], BF16, name="qb", align_bytes=64)
-        for h in range(2):
-            dst = qb[:, :, h * 64:(h + 1) * 64, :].rearrange("p r m j -> p m j r")
-            src = qraw[h][:].rearrange("p j (m r) -> p m j r", r=PACK)
-            nc.scalar.copy(dst, src)
-        skf = keep.tile([P, PACK, G], F32, name="skf")
-        skb = keep.tile([P, G, PACK], BF16, name="skb", tag="skb", align_bytes=64)
-        for t in range(PACK):
-            gat = keep.tile([P, G, PAGE], F32, name="gat%d" % t)
+        def spread():
+            tl["sgps"] = [ps([P, 4, G], "sgps%d" % a, ["red", "skT1"][a]) for a in range(2)]
+            for a in range(2):
+                for j in range(4):
+                    nc.tensor.transpose(tl["sgps"][a][:, j, :],
+                                        sg_col[:, 4 * a + j:4 * a + j + 1].to_broadcast([P, P]), ident[:])
+
+        def sgb_copy(on_vector):
+            tl["sgb"] = sb([P, G, PAGE], F32, "sgb")
+            nc.scalar.copy(tl["sgb"][:, :, 0:4], tl["sgps"][0][:].rearrange("p j g -> p g j"))
+            if on_vector:
+                nc.vector.tensor_copy(tl["sgb"][:, :, 4:8], tl["sgps"][1][:].rearrange("p j g -> p g j"))
+            else:
+                nc.scalar.copy(tl["sgb"][:, :, 4:8], tl["sgps"][1][:].rearrange("p j g -> p g j"))
+
+        def sgb3_copy():
+            tl["sgb3"] = sb([P, G, PAGE], F32, "sgb3")
+            for a in range(2):
+                nc.scalar.activation(tl["sgb3"][:, :, 4 * a:4 * a + 4], tl["sgps"][a][:].rearrange("p j g -> p g j"),
+                                     ACT.Copy, scale=dsc_sb[:, 3:4])
+
+        skf = sb([P, PACK, G], F32, "skf")
+
+        def gather(t, signs):
+            gat = sb([P, G, PAGE], F32, "gat%d" % t)
+            tl["gat", t] = gat
             gflat = gat[:].rearrange("p g j -> p (g j)")
             win = kt[t][:].indirect(offs_sb[:])
-            if PATHS[t] == 1:
-                nc.vector.tensor_tensor(gflat, win, sgb3[:].rearrange("p g j -> p (g j)"), ALU.mult)
-                nc.vector.tensor_reduce(skf[:, t, :], gat[:], AX.X, ALU.add)
-            elif PATHS[t] == 2:
-                nc.vector.tensor_tensor(gflat, win, sgb[:].rearrange("p g j -> p (g j)"), ALU.mult)
-                red = psum.tile([P, P], F32, name="red%d" % t, tag="r%d" % (t % 2))
-                for j in range(PAGE):
-                    nc.tensor.matmul(red[:], gat[:, :, j], ident[:], start=(j == 0), stop=(j == PAGE - 1),
-                                     is_transpose=True)
-                reds = keep.tile([P, P], F32, name="reds%d" % t, tag=("qraw1" if t == 2 else "reds%d" % t))
-                nc.scalar.copy(reds[:], red[:])
-                skT = psum.tile([P, G], F32, name="skT%d" % t, tag="skT")
-                nc.tensor.transpose(skT[:], reds[:], ident[:])
-                nc.scalar.activation(skf[:, t, :], skT[:], ACT.Copy, scale=dsc_sb[:, t:t + 1])
+            if signs is None:
+                nc.vector.tensor_copy(gflat, win)
+            else:
+                nc.vector.tensor_tensor(gflat, win, tl[signs][:].rearrange("p g j -> p (g j)"), ALU.mult)
 
-        qc = keep.tile([P, Q], U32, name="qc", align_bytes=64)
-        qs = keep.tile([P, Q], U8, name="qs", align_bytes=64)
-        nc.vector.quantize_mx(out=qc[:].bitcast(FP8X4), scales=qs[:], in_=qb[:].rearrange("p r m j -> p (r m j)"))
+        def vsum(t):
+            nc.vector.tensor_reduce(skf[:, t, :], tl["gat", t][:], AX.X, ALU.add)
 
-        nc.scalar.copy(skb[:].rearrange("p (c i) t -> p c t i", i=4), skf[:].rearrange("p t (c i) -> p c t i", i=4))
-        bg = [keep.tile([P, G], F32, name="bg%d" % r) for r in range(3)]
-        for r in range(3):
-            nc.vector.tensor_copy(bg[r][:], bt[r][:].indirect(offs2_sb[:]))
-        skc = keep.tile([P, G], U32, name="skc", align_bytes=64)
-        sks = keep.tile([P, G], U8, name="sks", align_bytes=64)
-        nc.vector.quantize_mx(out=skc[:].bitcast(FP8X4), scales=sks[:], in_=skb[:].rearrange("p g t -> p (g t)"))
-        bgl = keep.tile([P, 1, G], F32, name="bgl", tag="skb", align_bytes=64)
-        for r in range(3, PACK):
-            nc.vector.tensor_copy(bgl[:, r - 3, :], bt[r][:].indirect(offs2_sb[:]))
+        def pesum(t):
+            red = ps([P, P], "red%d" % t, "f3")
+            tl["red", t] = red
+            for j in range(PAGE):
+                nc.tensor.matmul(red[:], tl["gat", t][:, :, j], ident[:], start=(j == 0), stop=(j == PAGE - 1),
+                                 is_transpose=True)
 
-        acc = [psum.tile([P, G], F32, name="acc%d" % r, tag=["w0", "w1", "a2", "a3"][r]) for r in range(PACK)]
+        def peback(t):
+            reds = sb([P, P], F32, "reds%d" % t)
+            nc.scalar.copy(reds[:], tl["red", t][:])
+            skT = ps([P, G], "skT%d" % t, "skT%d" % (t % 2))
+            nc.tensor.transpose(skT[:], reds[:], ident[:])
+            nc.scalar.activation(skf[:, t, :], skT[:], ACT.Copy, scale=dsc_sb[:, t:t + 1])
+
+        def turn(t):
+            sc = sb([P, PAGE, P], F32, "sc%d" % t)
+            tl["sc", t] = sc
+            for a in range(4):
+                tp = ps([P, 2, P], "tp%d_%d" % (t, a), "f%d" % a)
+                for j in range(2):
+                    nc.tensor.transpose(tp[:, j, :], tl["gat", t][:, :, 2 * a + j], ident[:])
+                for j in range(2):
+                    jj = 2 * a + j
+                    nc.scalar.activation(sc[:, jj, :], tp[:, j, :], ACT.Copy, scale=sg_col[:, jj:jj + 1])
+
+        def turnback(t):
+            skT = ps([P, G], "skT%d" % t, "skT%d" % (t % 2))
+            for j in range(PAGE):
+                nc.tensor.matmul(skT[:], tl["sc", t][:, j, :], ident[:], start=(j == 0), stop=(j == PAGE - 1),
+                                 is_transpose=True)
+            nc.scalar.activation(skf[:, t, :], skT[:], ACT.Copy, scale=dsc_sb[:, t:t + 1])
+
+        def cast(h, eng):
+            if "qb" not in tl:
+                tl["qb"] = sb([P, PACK, P, PACK], BF16, "qb")
+            dst = tl["qb"][:, :, h * 64:(h + 1) * 64, :].rearrange("p r m j -> p m j r")
+            src = qraw[h][:].rearrange("p j (m r) -> p m j r", r=PACK)
+            if eng == "v":
+                nc.vector.tensor_copy(dst, src)
+            else:
+                nc.scalar.copy(dst, src)
+
+        qc = sb([P, Q], U32, "qc")
+        qs = sb([P, Q], U8, "qs")
+        skc = sb([P, G], U32, "skc")
+        sks = sb([P, G], U8, "sks")
+
+        def qquant():
+            nc.vector.quantize_mx(out=qc[:].bitcast(FP8X4), scales=qs[:],
+                                  in_=tl["qb"][:].rearrange("p r m j -> p (r m j)"))
+
+        def skweave(eng):
+            tl["skb"] = sb([P, G, PACK], BF16, "skb")
+            dst = tl["skb"][:].rearrange("p (c i) t -> p c t i", i=4)
+            src = skf[:].rearrange("p t (c i) -> p c t i", i=4)
+            if eng == "v":
+                nc.vector.tensor_copy(dst, src)
+            else:
+                nc.scalar.copy(dst, src)
+
+        def skquant():
+            nc.vector.quantize_mx(out=skc[:].bitcast(FP8X4), scales=sks[:],
+                                  in_=tl["skb"][:].rearrange("p g t -> p (g t)"))
+
+        def bgather(r):
+            bg = sb([P, G], F32, "bg%d" % r)
+            tl["bg", r] = bg
+            nc.vector.tensor_copy(bg[:], bt[r][:].indirect(offs2_sb[:]))
+
+        def clock(name, ap):
+            c = sb([P, 1], F32, name)
+            nc.gpsimd.tensor_copy(c[:], ap)
+
+        spread()
+        sgb_copy(False)
+        sgb3_copy()
+        gather(0, None)
+        turn(0)
+        turnback(0)
+        gather(1, None)
+        turn(1)
+        turnback(1)
+        gather(2, "sgb")
+        pesum(2)
+        cast(0, "s")
+        cast(1, "s")
+        peback(2)
+        gather(3, "sgb3")
+        vsum(3)
+        bgather(0)
+        bgather(1)
+        qquant()
+        skweave("s")
+        skquant()
+        bgather(2)
+        bgather(3)
+
+        acc = [ps([P, G], "acc%d" % r, "f%d" % r) for r in range(PACK)]
         for r in range(PACK):
             cols = slice(r * P, (r + 1) * P)
             nc.tensor.matmul_mx(out=acc[r][:], lhsT=qc[:, cols].bitcast(FP8X4), lhsT_scale=qs[:, cols],
                                 rhs=skc[:].bitcast(FP8X4), rhs_scale=sks[:], start=True, stop=True)
 
-        s = keep.tile([P, PACK, G], F32, name="s")
-        nmax = keep.tile([P, PACK], F32, name="nmax")
-        pe = keep.tile([P, PACK, G], F32, name="pe")
-        ssum = keep.tile([P, PACK], F32, name="ssum")
-        rinv = keep.tile([P, PACK], F32, name="rinv")
-        y = keep.tile([P, PACK, G], F32, name="y")
-        yb = keep.tile([P, G, PACK], BF16, name="yb", align_bytes=64)
-        yc = keep.tile([P, G], U32, name="yc", align_bytes=64)
-        ys = keep.tile([P, G], U8, name="ys", align_bytes=64)
+        s = sb([P, PACK, G], F32, "s")
+        nmax = sb([P, PACK], F32, "nmax")
+        pe = sb([P, PACK, G], F32, "pe")
+        ssum = sb([P, PACK], F32, "ssum")
+        rinv = sb([P, PACK], F32, "rinv")
+        y = sb([P, PACK, G], F32, "y")
+        yb = sb([P, G, PACK], BF16, "yb")
+        yc = sb([P, G], U32, "yc")
+        ys = sb([P, G], U8, "ys")
         for r in range(PACK + 1):
             if r < PACK:
-                nc.vector.tensor_tensor(s[:, r, :], acc[r][:], (bg[r][:] if r < 3 else bgl[:, r - 3, :]), ALU.add)
+                nc.vector.tensor_tensor(s[:, r, :], acc[r][:], tl["bg", r][:], ALU.add)
             if r > 0:
                 k = r - 1
                 nc.vector.tensor_reduce(nmax[:, k:k + 1], s[:, k, :], AX.X, ALU.max, negate=True)
                 nc.scalar.activation(pe[:, k, :], s[:, k, :], ACT.Exp, bias=nmax[:, k:k + 1],
                                      accum_out=ssum[:, k:k + 1])
-        out_v = out_0.rearrange("(p r) g -> p r g", r=PACK)
         for h in range(2):
             rr = slice(2 * h, 2 * h + 2)
             nc.vector.reciprocal(rinv[:, rr], ssum[:, rr])

@@ -20,7 +20,11 @@ AX = mybir.AxisListType
 P = 128
 PACK = 4
 PAGE = I // G
-TAGS = {"reds2":"qraw1","bg2":"skb","bg3":"gat3","qb":"sg_col"}
+LAST = PACK - 1
+LINE = 4
+HALF_Q = Q // 2
+HALF_M = P // 2
+OUT_SCALE = 128.0
 
 
 def tile_attend_pagesketch_pl_kernel(tc, query, keys, sg, dsc, bias, offs, offs2, out_0, out_1, out_2):
@@ -30,214 +34,167 @@ def tile_attend_pagesketch_pl_kernel(tc, query, keys, sg, dsc, bias, offs, offs2
         keep = ctx.enter_context(tc.tile_pool(name="keep", bufs=1))
         psum = ctx.enter_context(tc.psum_pool(name="psum", bufs=1))
 
-        def sb(shape, dtype, name):
-            return keep.tile(shape, dtype, name=name, tag=TAGS.get(name, name), align_bytes=64)
+        def sbuf(shape, dtype, name, tag=None):
+            return keep.tile(shape, dtype, name=name, tag=tag or name, align_bytes=64)
 
-        def ps(shape, name, tag):
+        def bank(shape, name, tag):
             return psum.tile(shape, F32, name=name, tag=tag)
 
-        keys_v = keys.rearrange("(p t) n -> p t n", t=PACK)
-        query_v = query.rearrange("(p t) n -> p t n", t=PACK)
-        bias_v = bias.rearrange("(p r) n -> p r n", r=PACK)
-        out_v = out_0.rearrange("(p r) g -> p r g", r=PACK)
+        keys_rows = keys.rearrange("(p t) n -> p t n", t=PACK)
+        query_rows = query.rearrange("(p t) n -> p t n", t=PACK)
+        bias_rows = bias.rearrange("(p r) n -> p r n", r=PACK)
+        out_rows = out_0.rearrange("(p r) g -> p r g", r=PACK)
 
-        kt = [sb([P, T], F32, "keys%d" % t) for t in range(PACK)]
-        offs_sb = lists.tile([P, I // 16], U16, name="offs_sb")
-        offs2_sb = lists.tile([P, G // 16], U16, name="offs2_sb")
-        sg_col = sb([P, PAGE], F32, "sg_col")
-        dsc_sb = sb([P, PACK], F32, "dsc_sb")
-        qraw = [sb([P, PACK, Q // 2], F32, "qraw%d" % h) for h in range(2)]
-        bt = [sb([P, U], F32, "bias%d" % r) for r in range(PACK)]
+        key_plane = [sbuf([P, T], F32, "keys%d" % t) for t in range(PACK)]
+        slot_list = lists.tile([P, I // 16], U16, name="slot_list")
+        page_list = lists.tile([P, G // 16], U16, name="page_list")
+        sg_page = sbuf([P, PAGE], F32, "sg_page")
+        dsc_sb = sbuf([P, PACK], F32, "dsc_sb")
+        query_raw = [sbuf([P, PACK, HALF_Q], F32, "query_raw%d" % h) for h in range(2)]
+        bias_tile = [sbuf([P, U], F32, "bias%d" % r) for r in range(PACK)]
 
-        nc.sync.dma_start(kt[0][:], keys_v[:, 0, :])
-        nc.sync.dma_start(offs_sb[:], offs)
-        nc.sync.dma_start(sg_col[:], sg.rearrange("o (p j) -> p (o j)", j=PAGE))
-        nc.sync.dma_start(dsc_sb[:], dsc.rearrange("(p t) o -> p (t o)", t=PACK))
-        nc.sync.dma_start(kt[1][:], keys_v[:, 1, :])
-        nc.sync.dma_start(kt[2][:], keys_v[:, 2, :])
-        nc.sync.dma_start(kt[3][:], keys_v[:, 3, :])
-        nc.sync.dma_start(offs2_sb[:], offs2)
-        nc.sync.dma_start(qraw[0][:], query_v[:, :, 0:256])
-        nc.sync.dma_start(qraw[1][:], query_v[:, :, 256:512])
-        nc.sync.dma_start(bt[0][:], bias_v[:, 0, :])
-        nc.sync.dma_start(bt[1][:], bias_v[:, 1, :])
-        nc.sync.dma_start(bt[2][:], bias_v[:, 2, :])
-        nc.sync.dma_start(bt[3][:], bias_v[:, 3, :])
+        nc.sync.dma_start(slot_list[:], offs)
+        nc.scalar.dma_start(sg_page[:], sg.rearrange("o (p j) -> p (o j)", j=PAGE))
+        nc.scalar.dma_start(dsc_sb[:], dsc.rearrange("(p t) o -> p (t o)", t=PACK))
+        for t in range(PACK):
+            nc.sync.dma_start(key_plane[t][:], keys_rows[:, t, :])
+        nc.sync.dma_start(page_list[:], offs2)
+        for h in range(2):
+            nc.sync.dma_start(query_raw[h][:], query_rows[:, :, h * HALF_Q:(h + 1) * HALF_Q])
+        for r in range(PACK):
+            nc.sync.dma_start(bias_tile[r][:], bias_rows[:, r, :])
 
-        ident = sb([P, P], F32, "ident")
+        ident = sbuf([P, P], F32, "ident")
         make_identity(nc, ident[:])
-        warm = sb([P, 1], F32, "warm")
-        nc.scalar.activation(warm[:], ident[:, 0:1], ACT.Exp)
 
-        tl = {}
+        sg_bank = [bank([P, LINE, G], "sg_bank%d" % a, "sum%d" % (a + 1)) for a in range(2)]
+        for j in range(PAGE):
+            nc.tensor.transpose(sg_bank[j // LINE][:, j % LINE, :], sg_page[:, j:j + 1].to_broadcast([P, P]), ident[:])
+        sg_row = sbuf([P, G, PAGE], F32, "sg_row")
+        for a in range(2):
+            nc.scalar.copy(sg_row[:, :, LINE * a:LINE * (a + 1)], sg_bank[a][:].rearrange("p j g -> p g j"))
+        sg_dsc_row = sbuf([P, G, PAGE], F32, "sg_dsc_row")
+        for a in range(2):
+            nc.scalar.activation(sg_dsc_row[:, :, LINE * a:LINE * (a + 1)], sg_bank[a][:].rearrange("p j g -> p g j"),
+                                 ACT.Copy, scale=dsc_sb[:, LAST:LAST + 1])
 
-        def spread():
-            tl["sgps"] = [ps([P, 4, G], "sgps%d" % a, ["red", "skT1"][a]) for a in range(2)]
-            for a in range(2):
-                for j in range(4):
-                    nc.tensor.transpose(tl["sgps"][a][:, j, :],
-                                        sg_col[:, 4 * a + j:4 * a + j + 1].to_broadcast([P, P]), ident[:])
+        sums = bank([P, LAST, G], "sums", "sums")
+        sk_bf = sbuf([P, G, PACK], BF16, "sk_bf")
 
-        def sgb_copy(on_vector):
-            tl["sgb"] = sb([P, G, PAGE], F32, "sgb")
-            nc.scalar.copy(tl["sgb"][:, :, 0:4], tl["sgps"][0][:].rearrange("p j g -> p g j"))
-            if on_vector:
-                nc.vector.tensor_copy(tl["sgb"][:, :, 4:8], tl["sgps"][1][:].rearrange("p j g -> p g j"))
+        def gather_keys(t, factor):
+            picked = sbuf([P, G, PAGE], F32, "picked%d" % t)
+            flat = picked[:].rearrange("p g j -> p (g j)")
+            window = key_plane[t][:].indirect(slot_list[:])
+            if factor is None:
+                nc.vector.tensor_copy(flat, window)
             else:
-                nc.scalar.copy(tl["sgb"][:, :, 4:8], tl["sgps"][1][:].rearrange("p j g -> p g j"))
+                nc.vector.tensor_tensor(flat, window, factor[:].rearrange("p g j -> p (g j)"), ALU.mult)
+            return picked
 
-        def sgb3_copy():
-            tl["sgb3"] = sb([P, G, PAGE], F32, "sgb3")
-            for a in range(2):
-                nc.scalar.activation(tl["sgb3"][:, :, 4 * a:4 * a + 4], tl["sgps"][a][:].rearrange("p j g -> p g j"),
-                                     ACT.Copy, scale=dsc_sb[:, 3:4])
-
-        skf = sb([P, PACK, G], F32, "skf")
-
-        def gather(t, signs):
-            gat = sb([P, G, PAGE], F32, "gat%d" % t)
-            tl["gat", t] = gat
-            gflat = gat[:].rearrange("p g j -> p (g j)")
-            win = kt[t][:].indirect(offs_sb[:])
-            if signs is None:
-                nc.vector.tensor_copy(gflat, win)
-            else:
-                nc.vector.tensor_tensor(gflat, win, tl[signs][:].rearrange("p g j -> p (g j)"), ALU.mult)
-
-        def vsum(t):
-            nc.vector.tensor_reduce(skf[:, t, :], tl["gat", t][:], AX.X, ALU.add)
-
-        def pesum(t):
-            red = ps([P, P], "red%d" % t, "f3")
-            tl["red", t] = red
+        def add_turned(out, slots):
             for j in range(PAGE):
-                nc.tensor.matmul(red[:], tl["gat", t][:, :, j], ident[:], start=(j == 0), stop=(j == PAGE - 1),
-                                 is_transpose=True)
+                nc.tensor.matmul(out, slots[j], ident[:], start=(j == 0), stop=(j == PAGE - 1), is_transpose=True)
 
-        def peback(t):
-            reds = sb([P, P], F32, "reds%d" % t)
-            nc.scalar.copy(reds[:], tl["red", t][:])
-            skT = ps([P, G], "skT%d" % t, "skT%d" % (t % 2))
-            nc.tensor.transpose(skT[:], reds[:], ident[:])
-            nc.scalar.activation(skf[:, t, :], skT[:], ACT.Copy, scale=dsc_sb[:, t:t + 1])
+        def sum_pages(t, picked):
+            turned = bank([P, P], "turned%d" % t, "sum%d" % t)
+            add_turned(turned[:], [picked[:, :, j] for j in range(PAGE)])
+            return turned
 
-        def turn(t):
-            sc = sb([P, PAGE, P], F32, "sc%d" % t)
-            tl["sc", t] = sc
-            for a in range(4):
-                tp = ps([P, 2, P], "tp%d_%d" % (t, a), "f%d" % a)
-                for j in range(2):
-                    nc.tensor.transpose(tp[:, j, :], tl["gat", t][:, :, 2 * a + j], ident[:])
-                for j in range(2):
-                    jj = 2 * a + j
-                    nc.scalar.activation(sc[:, jj, :], tp[:, j, :], ACT.Copy, scale=sg_col[:, jj:jj + 1])
+        def turn_back(t, turned):
+            staged = sbuf([P, P], F32, "staged%d" % t)
+            nc.scalar.copy(staged[:], turned[:])
+            nc.tensor.transpose(sums[:, t, :], staged[:], ident[:])
 
-        def turnback(t):
-            skT = ps([P, G], "skT%d" % t, "skT%d" % (t % 2))
-            for j in range(PAGE):
-                nc.tensor.matmul(skT[:], tl["sc", t][:, j, :], ident[:], start=(j == 0), stop=(j == PAGE - 1),
-                                 is_transpose=True)
-            nc.scalar.activation(skf[:, t, :], skT[:], ACT.Copy, scale=dsc_sb[:, t:t + 1])
+        picked0 = gather_keys(0, None)
+        signed0 = sbuf([P, PAGE, P], F32, "signed0")
+        for a in range(PAGE // 2):
+            pair = bank([P, 2, P], "pair%d" % a, "ring%d" % a)
+            for e in range(2):
+                nc.tensor.transpose(pair[:, e, :], picked0[:, :, 2 * a + e], ident[:])
+            for e in range(2):
+                j = 2 * a + e
+                nc.scalar.activation(signed0[:, j, :], pair[:, e, :], ACT.Copy, scale=sg_page[:, j:j + 1])
+        add_turned(sums[:, 0, :], [signed0[:, j, :] for j in range(PAGE)])
 
-        def cast(h, eng):
-            if "qb" not in tl:
-                tl["qb"] = sb([P, PACK, P, PACK], BF16, "qb")
-            dst = tl["qb"][:, :, h * 64:(h + 1) * 64, :].rearrange("p r m j -> p m j r")
-            src = qraw[h][:].rearrange("p j (m r) -> p m j r", r=PACK)
-            if eng == "v":
-                nc.vector.tensor_copy(dst, src)
-            else:
-                nc.scalar.copy(dst, src)
+        picked1 = gather_keys(1, sg_row)
+        turn_back(1, sum_pages(1, picked1))
+        picked2 = gather_keys(2, sg_row)
+        turned2 = sum_pages(2, picked2)
 
-        qc = sb([P, Q], U32, "qc")
-        qs = sb([P, Q], U8, "qs")
-        skc = sb([P, G], U32, "skc")
-        sks = sb([P, G], U8, "sks")
+        query_bf = sbuf([P, PACK, P, PACK], BF16, "query_bf", tag="picked1")
 
-        def qquant():
-            nc.vector.quantize_mx(out=qc[:].bitcast(FP8X4), scales=qs[:],
-                                  in_=tl["qb"][:].rearrange("p r m j -> p (r m j)"))
+        def round_query(h):
+            nc.scalar.copy(query_bf[:, :, h * HALF_M:(h + 1) * HALF_M, :].rearrange("p r m t -> p m t r"),
+                           query_raw[h][:].rearrange("p t (m r) -> p m t r", r=PACK))
 
-        def skweave(eng):
-            tl["skb"] = sb([P, G, PACK], BF16, "skb")
-            dst = tl["skb"][:].rearrange("p (c i) t -> p c t i", i=4)
-            src = skf[:].rearrange("p t (c i) -> p c t i", i=4)
-            if eng == "v":
-                nc.vector.tensor_copy(dst, src)
-            else:
-                nc.scalar.copy(dst, src)
+        round_query(0)
+        turn_back(2, turned2)
+        round_query(1)
 
-        def skquant():
-            nc.vector.quantize_mx(out=skc[:].bitcast(FP8X4), scales=sks[:],
-                                  in_=tl["skb"][:].rearrange("p g t -> p (g t)"))
+        picked3 = gather_keys(LAST, sg_dsc_row)
+        with nc.allow_low_precision(reason="the sum is float32; its result is rounded once, for the quantiser"):
+            nc.vector.tensor_reduce(sk_bf[:, :, LAST], picked3[:], AX.X, ALU.add)
 
-        def bgather(r):
-            bg = sb([P, G], F32, "bg%d" % r)
-            tl["bg", r] = bg
-            nc.vector.tensor_copy(bg[:], bt[r][:].indirect(offs2_sb[:]))
+        def gather_bias(r, out):
+            nc.vector.tensor_copy(out, bias_tile[r][:].indirect(page_list[:]))
+            return out
 
-        def clock(name, ap):
-            c = sb([P, 1], F32, name)
-            nc.gpsimd.tensor_copy(c[:], ap)
+        query_codes = sbuf([P, Q], U32, "query_codes")
+        query_scales = sbuf([P, Q], U8, "query_scales")
+        sk_codes = sbuf([P, G], U32, "sk_codes")
+        sk_scales = sbuf([P, G], U8, "sk_scales")
 
-        spread()
-        sgb_copy(False)
-        sgb3_copy()
-        gather(0, None)
-        turn(0)
-        turnback(0)
-        gather(1, None)
-        turn(1)
-        turnback(1)
-        gather(2, "sgb")
-        pesum(2)
-        cast(0, "s")
-        cast(1, "s")
-        peback(2)
-        gather(3, "sgb3")
-        vsum(3)
-        bgather(0)
-        bgather(1)
-        qquant()
-        skweave("s")
-        skquant()
-        bgather(2)
-        bgather(3)
+        bias0 = sbuf([P, G], F32, "bias_picked0")
+        bias_picked = [gather_bias(0, bias0[:])]
+        nc.vector.tensor_tensor(sk_bf[:, :, 0:LAST], sums[:].rearrange("p t g -> p g t"),
+                                dsc_sb[:, 0:LAST].unsqueeze(1).to_broadcast([P, G, LAST]), ALU.mult)
+        nc.vector.quantize_mx(out=query_codes[:].bitcast(FP8X4), scales=query_scales[:],
+                              in_=query_bf[:].rearrange("p r m t -> p (r m t)"))
+        nc.vector.quantize_mx(out=sk_codes[:].bitcast(FP8X4), scales=sk_scales[:],
+                              in_=sk_bf[:].rearrange("p g t -> p (g t)"))
+        bias1 = sbuf([P, G], F32, "bias_picked1", tag="picked1")
+        bias_picked.append(gather_bias(1, bias1[:]))
+        bias23 = sbuf([P, 2, G], F32, "bias_picked23", tag="sk_bf")
+        for e in range(2):
+            bias_picked.append(gather_bias(2 + e, bias23[:, e, :]))
 
-        acc = [ps([P, G], "acc%d" % r, "f%d" % r) for r in range(PACK)]
+        scores = [bank([P, G], "scores%d" % r, "ring%d" % r) for r in range(PACK)]
         for r in range(PACK):
             cols = slice(r * P, (r + 1) * P)
-            nc.tensor.matmul_mx(out=acc[r][:], lhsT=qc[:, cols].bitcast(FP8X4), lhsT_scale=qs[:, cols],
-                                rhs=skc[:].bitcast(FP8X4), rhs_scale=sks[:], start=True, stop=True)
+            nc.tensor.matmul_mx(out=scores[r][:], lhsT=query_codes[:, cols].bitcast(FP8X4),
+                                lhsT_scale=query_scales[:, cols], rhs=sk_codes[:].bitcast(FP8X4),
+                                rhs_scale=sk_scales[:], start=True, stop=True)
 
-        s = sb([P, PACK, G], F32, "s")
-        nmax = sb([P, PACK], F32, "nmax")
-        pe = sb([P, PACK, G], F32, "pe")
-        ssum = sb([P, PACK], F32, "ssum")
-        rinv = sb([P, PACK], F32, "rinv")
-        y = sb([P, PACK, G], F32, "y")
-        yb = sb([P, G, PACK], BF16, "yb")
-        yc = sb([P, G], U32, "yc")
-        ys = sb([P, G], U8, "ys")
-        for r in range(PACK + 1):
-            if r < PACK:
-                nc.vector.tensor_tensor(s[:, r, :], acc[r][:], tl["bg", r][:], ALU.add)
-            if r > 0:
-                k = r - 1
-                nc.vector.tensor_reduce(nmax[:, k:k + 1], s[:, k, :], AX.X, ALU.max, negate=True)
-                nc.scalar.activation(pe[:, k, :], s[:, k, :], ACT.Exp, bias=nmax[:, k:k + 1],
-                                     accum_out=ssum[:, k:k + 1])
+        s = sbuf([P, PACK, G], F32, "s")
+        neg_max = sbuf([P, PACK], F32, "neg_max")
+        weights = sbuf([P, PACK, G], F32, "weights")
+        row_sum = sbuf([P, PACK], F32, "row_sum")
+        inv_sum = sbuf([P, PACK], F32, "inv_sum")
+        y = sbuf([P, PACK, G], F32, "y")
+        y_bf = sbuf([P, G, PACK], BF16, "y_bf")
+        y_codes = sbuf([P, G], U32, "y_codes")
+        y_scales = sbuf([P, G], U8, "y_scales")
+
+        for step in range(PACK + 1):
+            if step < PACK:
+                nc.vector.tensor_tensor(s[:, step, :], scores[step][:], bias_picked[step], ALU.add)
+            if step > 0:
+                r = step - 1
+                nc.vector.tensor_reduce(neg_max[:, r:r + 1], s[:, r, :], AX.X, ALU.max, negate=True)
+                nc.scalar.activation(weights[:, r, :], s[:, r, :], ACT.Exp, bias=neg_max[:, r:r + 1],
+                                     accum_out=row_sum[:, r:r + 1])
         for h in range(2):
-            rr = slice(2 * h, 2 * h + 2)
-            nc.vector.reciprocal(rinv[:, rr], ssum[:, rr])
-            nc.vector.scalar_tensor_tensor(yb[:, :, rr], pe[:, rr, :].rearrange("p r g -> p g r"), 128.0,
-                                           rinv[:, rr].unsqueeze(1).to_broadcast([P, G, 2]), ALU.mult, ALU.mult)
+            two = slice(2 * h, 2 * h + 2)
+            nc.vector.reciprocal(inv_sum[:, two], row_sum[:, two])
+            nc.vector.scalar_tensor_tensor(y_bf[:, :, two], weights[:, two, :].rearrange("p r g -> p g r"), OUT_SCALE,
+                                           inv_sum[:, two].unsqueeze(1).to_broadcast([P, G, 2]), ALU.mult, ALU.mult)
             for r in range(2 * h, 2 * h + 2):
-                nc.vector.tensor_scalar(y[:, r, :], pe[:, r, :], 128.0, rinv[:, r:r + 1], ALU.mult, ALU.mult)
-            nc.sync.dma_start(out_v[:, rr, :], y[:, rr, :])
-        nc.vector.quantize_mx(out=yc[:].bitcast(FP8X4), scales=ys[:], in_=yb[:].rearrange("p g r -> p (g r)"))
+                nc.vector.tensor_scalar(y[:, r, :], weights[:, r, :], OUT_SCALE, inv_sum[:, r:r + 1], ALU.mult, ALU.mult)
+            nc.sync.dma_start(out_rows[:, two, :], y[:, two, :])
+        nc.vector.quantize_mx(out=y_codes[:].bitcast(FP8X4), scales=y_scales[:],
+                              in_=y_bf[:].rearrange("p g r -> p (g r)"))
 
-        nc.scalar.dma_start(out_1.rearrange("z l c r -> l (z c r)").bitcast(I32), yc[:].bitcast(I32))
-        for k in range(4):
-            eng = nc.sync if k % 2 == 0 else nc.scalar
-            eng.dma_start(out_2[0, 4 * k:4 * k + 4, :].bitcast(I32), ys[32 * k:32 * k + 4, :].bitcast(I32))
+        nc.scalar.dma_start(out_1.rearrange("z l c r -> l (z c r)").bitcast(I32), y_codes[:].bitcast(I32))
+        for k in range(P // 32):
+            queue = nc.sync if k % 2 == 0 else nc.scalar
+            queue.dma_start(out_2[0, 4 * k:4 * k + 4, :].bitcast(I32), y_scales[32 * k:32 * k + 4, :].bitcast(I32))

from contextlib import ExitStack

import concourse.mybir as mybir
from concourse.masks import make_identity

D, T, I, G, U, Q = 512, 2048, 1024, 128, 512, 512
FLOPS = 2 * D * Q * G

F32 = mybir.dt.float32
BF16 = mybir.dt.bfloat16
U32 = mybir.dt.uint32
U16 = mybir.dt.uint16
I32 = mybir.dt.int32
U8 = mybir.dt.uint8
FP8X4 = mybir.dt.float8_e4m3fn_x4
ALU = mybir.AluOpType
ACT = mybir.ActivationFunctionType
AX = mybir.AxisListType

P = 128
PACK = 4
PAGE = I // G
LAST = PACK - 1
LINE = 4
HALF_Q = Q // 2
HALF_M = P // 2
OUT_SCALE = 128.0


def tile_attend_pagesketch_pl_kernel(tc, query, keys, sg, dsc, bias, offs, offs2, out_0, out_1, out_2):
    nc = tc.nc
    with ExitStack() as ctx:
        lists = ctx.enter_context(tc.tile_pool(name="lists", bufs=1))
        keep = ctx.enter_context(tc.tile_pool(name="keep", bufs=1))
        psum = ctx.enter_context(tc.psum_pool(name="psum", bufs=1))

        def sbuf(shape, dtype, name, tag=None):
            return keep.tile(shape, dtype, name=name, tag=tag or name, align_bytes=64)

        def bank(shape, name, tag):
            return psum.tile(shape, F32, name=name, tag=tag)

        keys_rows = keys.rearrange("(p t) n -> p t n", t=PACK)
        query_rows = query.rearrange("(p t) n -> p t n", t=PACK)
        bias_rows = bias.rearrange("(p r) n -> p r n", r=PACK)
        out_rows = out_0.rearrange("(p r) g -> p r g", r=PACK)

        key_plane = [sbuf([P, T], F32, "keys%d" % t) for t in range(PACK)]
        slot_list = lists.tile([P, I // 16], U16, name="slot_list")
        page_list = lists.tile([P, G // 16], U16, name="page_list")
        sg_page = sbuf([P, PAGE], F32, "sg_page")
        dsc_sb = sbuf([P, PACK], F32, "dsc_sb")
        query_raw = [sbuf([P, PACK, HALF_Q], F32, "query_raw%d" % h) for h in range(2)]
        bias_tile = [sbuf([P, U], F32, "bias%d" % r) for r in range(PACK)]

        nc.sync.dma_start(slot_list[:], offs)
        nc.scalar.dma_start(sg_page[:], sg.rearrange("o (p j) -> p (o j)", j=PAGE))
        nc.scalar.dma_start(dsc_sb[:], dsc.rearrange("(p t) o -> p (t o)", t=PACK))
        for t in range(PACK):
            nc.sync.dma_start(key_plane[t][:], keys_rows[:, t, :])
        nc.sync.dma_start(page_list[:], offs2)
        for h in range(2):
            nc.sync.dma_start(query_raw[h][:], query_rows[:, :, h * HALF_Q:(h + 1) * HALF_Q])
        for r in range(PACK):
            nc.sync.dma_start(bias_tile[r][:], bias_rows[:, r, :])

        ident = sbuf([P, P], F32, "ident")
        make_identity(nc, ident[:])

        sg_bank = [bank([P, LINE, G], "sg_bank%d" % a, "sum%d" % (a + 1)) for a in range(2)]
        for j in range(PAGE):
            nc.tensor.transpose(sg_bank[j // LINE][:, j % LINE, :], sg_page[:, j:j + 1].to_broadcast([P, P]), ident[:])
        sg_row = sbuf([P, G, PAGE], F32, "sg_row")
        for a in range(2):
            nc.scalar.copy(sg_row[:, :, LINE * a:LINE * (a + 1)], sg_bank[a][:].rearrange("p j g -> p g j"))
        sg_dsc_row = sbuf([P, G, PAGE], F32, "sg_dsc_row")
        for a in range(2):
            nc.scalar.activation(sg_dsc_row[:, :, LINE * a:LINE * (a + 1)], sg_bank[a][:].rearrange("p j g -> p g j"),
                                 ACT.Copy, scale=dsc_sb[:, LAST:LAST + 1])

        sums = bank([P, LAST, G], "sums", "sums")
        sk_bf = sbuf([P, G, PACK], BF16, "sk_bf")

        def gather_keys(t, factor):
            picked = sbuf([P, G, PAGE], F32, "picked%d" % t)
            flat = picked[:].rearrange("p g j -> p (g j)")
            window = key_plane[t][:].indirect(slot_list[:])
            if factor is None:
                nc.vector.tensor_copy(flat, window)
            else:
                nc.vector.tensor_tensor(flat, window, factor[:].rearrange("p g j -> p (g j)"), ALU.mult)
            return picked

        def add_turned(out, slots):
            for j in range(PAGE):
                nc.tensor.matmul(out, slots[j], ident[:], start=(j == 0), stop=(j == PAGE - 1), is_transpose=True)

        def sum_pages(t, picked):
            turned = bank([P, P], "turned%d" % t, "sum%d" % t)
            add_turned(turned[:], [picked[:, :, j] for j in range(PAGE)])
            return turned

        def turn_back(t, turned):
            staged = sbuf([P, P], F32, "staged%d" % t)
            nc.scalar.copy(staged[:], turned[:])
            nc.tensor.transpose(sums[:, t, :], staged[:], ident[:])

        picked0 = gather_keys(0, None)
        signed0 = sbuf([P, PAGE, P], F32, "signed0")
        for a in range(PAGE // 2):
            pair = bank([P, 2, P], "pair%d" % a, "ring%d" % a)
            for e in range(2):
                nc.tensor.transpose(pair[:, e, :], picked0[:, :, 2 * a + e], ident[:])
            for e in range(2):
                j = 2 * a + e
                nc.scalar.activation(signed0[:, j, :], pair[:, e, :], ACT.Copy, scale=sg_page[:, j:j + 1])
        add_turned(sums[:, 0, :], [signed0[:, j, :] for j in range(PAGE)])

        picked1 = gather_keys(1, sg_row)
        turn_back(1, sum_pages(1, picked1))
        picked2 = gather_keys(2, sg_row)
        turned2 = sum_pages(2, picked2)

        query_bf = sbuf([P, PACK, P, PACK], BF16, "query_bf", tag="picked1")

        def round_query(h):
            nc.scalar.copy(query_bf[:, :, h * HALF_M:(h + 1) * HALF_M, :].rearrange("p r m t -> p m t r"),
                           query_raw[h][:].rearrange("p t (m r) -> p m t r", r=PACK))

        round_query(0)
        turn_back(2, turned2)
        round_query(1)

        picked3 = gather_keys(LAST, sg_dsc_row)
        with nc.allow_low_precision(reason="the sum is float32; its result is rounded once, for the quantiser"):
            nc.vector.tensor_reduce(sk_bf[:, :, LAST], picked3[:], AX.X, ALU.add)

        def gather_bias(r, out):
            nc.vector.tensor_copy(out, bias_tile[r][:].indirect(page_list[:]))
            return out

        query_codes = sbuf([P, Q], U32, "query_codes")
        query_scales = sbuf([P, Q], U8, "query_scales")
        sk_codes = sbuf([P, G], U32, "sk_codes")
        sk_scales = sbuf([P, G], U8, "sk_scales")

        bias0 = sbuf([P, G], F32, "bias_picked0")
        bias_picked = [gather_bias(0, bias0[:])]
        nc.vector.tensor_tensor(sk_bf[:, :, 0:LAST], sums[:].rearrange("p t g -> p g t"),
                                dsc_sb[:, 0:LAST].unsqueeze(1).to_broadcast([P, G, LAST]), ALU.mult)
        nc.vector.quantize_mx(out=query_codes[:].bitcast(FP8X4), scales=query_scales[:],
                              in_=query_bf[:].rearrange("p r m t -> p (r m t)"))
        nc.vector.quantize_mx(out=sk_codes[:].bitcast(FP8X4), scales=sk_scales[:],
                              in_=sk_bf[:].rearrange("p g t -> p (g t)"))
        bias1 = sbuf([P, G], F32, "bias_picked1", tag="picked1")
        bias_picked.append(gather_bias(1, bias1[:]))
        bias23 = sbuf([P, 2, G], F32, "bias_picked23", tag="sk_bf")
        for e in range(2):
            bias_picked.append(gather_bias(2 + e, bias23[:, e, :]))

        scores = [bank([P, G], "scores%d" % r, "ring%d" % r) for r in range(PACK)]
        for r in range(PACK):
            cols = slice(r * P, (r + 1) * P)
            nc.tensor.matmul_mx(out=scores[r][:], lhsT=query_codes[:, cols].bitcast(FP8X4),
                                lhsT_scale=query_scales[:, cols], rhs=sk_codes[:].bitcast(FP8X4),
                                rhs_scale=sk_scales[:], start=True, stop=True)

        s = sbuf([P, PACK, G], F32, "s")
        neg_max = sbuf([P, PACK], F32, "neg_max")
        weights = sbuf([P, PACK, G], F32, "weights")
        row_sum = sbuf([P, PACK], F32, "row_sum")
        inv_sum = sbuf([P, PACK], F32, "inv_sum")
        y = sbuf([P, PACK, G], F32, "y")
        y_bf = sbuf([P, G, PACK], BF16, "y_bf")
        y_codes = sbuf([P, G], U32, "y_codes")
        y_scales = sbuf([P, G], U8, "y_scales")

        for step in range(PACK + 1):
            if step < PACK:
                nc.vector.tensor_tensor(s[:, step, :], scores[step][:], bias_picked[step], ALU.add)
            if step > 0:
                r = step - 1
                nc.vector.tensor_reduce(neg_max[:, r:r + 1], s[:, r, :], AX.X, ALU.max, negate=True)
                nc.scalar.activation(weights[:, r, :], s[:, r, :], ACT.Exp, bias=neg_max[:, r:r + 1],
                                     accum_out=row_sum[:, r:r + 1])
        for h in range(2):
            two = slice(2 * h, 2 * h + 2)
            nc.vector.reciprocal(inv_sum[:, two], row_sum[:, two])
            nc.vector.scalar_tensor_tensor(y_bf[:, :, two], weights[:, two, :].rearrange("p r g -> p g r"), OUT_SCALE,
                                           inv_sum[:, two].unsqueeze(1).to_broadcast([P, G, 2]), ALU.mult, ALU.mult)
            for r in range(2 * h, 2 * h + 2):
                nc.vector.tensor_scalar(y[:, r, :], weights[:, r, :], OUT_SCALE, inv_sum[:, r:r + 1], ALU.mult, ALU.mult)
            nc.sync.dma_start(out_rows[:, two, :], y[:, two, :])
        nc.vector.quantize_mx(out=y_codes[:].bitcast(FP8X4), scales=y_scales[:],
                              in_=y_bf[:].rearrange("p g r -> p (g r)"))

        nc.scalar.dma_start(out_1.rearrange("z l c r -> l (z c r)").bitcast(I32), y_codes[:].bitcast(I32))
        for k in range(P // 32):
            queue = nc.sync if k % 2 == 0 else nc.scalar
            queue.dma_start(out_2[0, 4 * k:4 * k + 4, :].bitcast(I32), y_scales[32 * k:32 * k + 4, :].bitcast(I32))
